import numpy as np
import ml_dtypes


def mxq(x, axis, fmt="e4m3"):
    dtype, down = {"e4m3": (ml_dtypes.float8_e4m3fn, 7), "e5m2": (ml_dtypes.float8_e5m2, 14)}[fmt]
    v = np.moveaxis(np.asarray(x, np.float32).astype(ml_dtypes.bfloat16).astype(np.float64), axis, -1)
    blocks = v.reshape(v.shape[:-1] + (-1, 32))
    amax = np.abs(blocks).max(-1, keepdims=True)
    byte = np.maximum(np.where(amax > 0, np.frexp(amax)[1] - 1 + 127, 0) - down, 1)
    scale = np.exp2(byte - 127.0)
    codes = (blocks / scale).astype(np.float32).astype(dtype).astype(np.float64)
    return np.moveaxis((codes * scale).reshape(v.shape), -1, axis)


WIDE = False


def mx_kscale(k):
    if not WIDE:
        return np.ones(k)
    levels = np.array([10, -10, 5, -5, 0])
    if k % 512:
        return np.exp2(np.random.permutation(np.resize(levels, k // 32))).repeat(32)
    a = np.empty((k // 512, 16))
    for p in range(k // 512):
        a[p, :8] = np.random.permutation(np.resize(levels, 8))
        for g in range(8):
            far = levels[np.abs(levels - a[p, g]) >= 10]
            a[p, g + 8] = far[np.random.randint(len(far))]
    return np.exp2(a.ravel()).repeat(32)


def f64(x):
    return np.asarray(x).astype(np.float64)


def striped(idx):
    return np.tile(np.asarray(idx).reshape(-1, 16).T, (8, 1)).astype(np.uint16)


def unstriped(offs):
    return offs[:16].T.reshape(-1).astype(np.int64)


E2M1 = np.array([0.0, 0.5, 1.0, 1.5, 2.0, 3.0, 4.0, 6.0, -0.0, -0.5, -1.0, -1.5, -2.0, -3.0, -4.0, -6.0])


def pack_weight(w, fmt):
    k, n = w.shape
    w = f64(np.asarray(w, np.float32).astype(ml_dtypes.bfloat16)).reshape(k // 32, 32, n)
    amax = np.abs(w).max(1)
    if fmt == "e4m3":
        byte = np.frexp(amax)[1] - 1 + 127 - 7
    else:
        mant, ex = np.frexp(amax / 6.0)
        byte = np.where(mant > 0.5, ex, ex - 1) + 127
    byte = np.clip(np.where(amax > 0, byte, 1), 1, 254)
    scaled = (w * np.exp2(127.0 - byte)[:, None, :]).reshape(k, n).astype(np.float32)
    by_word = np.ascontiguousarray(scaled.reshape(k // 512, 128, 4, n).transpose(0, 1, 3, 2))
    if fmt == "e4m3":
        words = by_word.astype(ml_dtypes.float8_e4m3fn).view(np.uint8)
    else:
        c = by_word.astype(ml_dtypes.float4_e2m1fn).view(np.uint8) & 0xF
        words = (c[..., 0::2] | (c[..., 1::2] << 4)).reshape(k // 512, 128, 2 * n)
    return np.ascontiguousarray(words), np.ascontiguousarray(byte.astype(np.uint8).reshape(k // 512, 16, n))


def unpack_weight(words, scales, fmt):
    g, _, n = scales.shape
    words = np.ascontiguousarray(words).reshape(g, 128, n, -1)
    if fmt == "e4m3":
        vals = words.view(ml_dtypes.float8_e4m3fn).astype(np.float64)
    else:
        nib = np.empty((g, 128, n, 4), np.uint8)
        nib[..., 0::2] = words & 0xF
        nib[..., 1::2] = words >> 4
        vals = E2M1[nib]
    vals = vals * np.repeat(np.exp2(scales.astype(np.float64) - 127.0), 8, axis=1)[..., None]
    return vals.transpose(0, 1, 3, 2).reshape(g * 512, n)


def bf(x):
    return np.asarray(x, np.float32).astype(ml_dtypes.bfloat16)


def planes(Y):
    r, m = Y.shape
    b = f64(bf(Y)).reshape(r // 32, 32, m)
    amax = np.abs(b).max(1)
    byte = np.clip(np.where(amax > 0, np.frexp(amax)[1] - 1 + 127 - 7, 1), 1, 254)
    codes = (b * np.exp2(127.0 - byte)[:, None, :]).reshape(r, m).astype(np.float32).astype(ml_dtypes.float8_e4m3fn).view(np.uint8)
    words = codes.reshape(r // 512, 128, 4, m).transpose(0, 1, 3, 2)
    return np.ascontiguousarray(words), np.ascontiguousarray(byte.astype(np.uint8).reshape(r // 512, 16, m))


K, T, J, N = 512, 2048, 512, 512


def setup_inputs():
    n = np.random.standard_normal
    idx = np.random.permutation(T)[:J]
    fk = mx_kscale(K)
    wap = pack_weight(n((K, N)) * 1 / np.sqrt(K) * fk[:, None], "e4m3")
    wbp = pack_weight(n((K, N)) * 1 / np.sqrt(K) * fk[:, None], "e2m1")
    return {
        "xf": (n((K, T))).astype(np.float32),
        "lo": (np.random.uniform(-1.2, -0.4, (K, 1))).astype(np.float32),
        "hi": (np.random.uniform(0.4, 1.2, (K, 1))).astype(np.float32),
        "fa": (np.random.uniform(0.5, 2.0, (K, 1)) / fk[:, None]).astype(np.float32),
        "fb": (np.random.uniform(0.5, 2.0, (K, 1)) / fk[:, None]).astype(np.float32),
        "wa_words": wap[0],
        "wa_scales": wap[1],
        "wb_words": wbp[0],
        "wb_scales": wbp[1],
        "offs": striped(idx),
    }


def reference(xf, lo, hi, fa, fb, wa_words, wa_scales, wb_words, wb_scales, offs):
    idx = unstriped(offs)
    wau = unpack_weight(wa_words, wa_scales, "e4m3")
    wbu = unpack_weight(wb_words, wb_scales, "e2m1")
    b = np.maximum(np.minimum(f64(xf)[:, idx], f64(hi)), f64(lo))
    xa = b * f64(fa)
    xc = (f64(xf)[:, idx] - b) * f64(fb)
    xaq = mxq(xa, 0, "e4m3")
    xcq = mxq(xc, 0, "e4m3")
    y = wau.T @ xaq + wbu.T @ xcq
    words, scales = planes(y)
    return y, words, scales

@@ -1,0 +1,162 @@
+from contextlib import ExitStack
+
+import concourse.mybir as mybir
+
+K, T, J, N = 512, 2048, 512, 512
+FLOPS = 2 * 2 * K * N * J
+
+F32 = mybir.dt.float32
+BF16 = mybir.dt.bfloat16
+I32 = mybir.dt.int32
+U32 = mybir.dt.uint32
+U16 = mybir.dt.uint16
+U8 = mybir.dt.uint8
+FP8X4 = mybir.dt.float8_e4m3fn_x4
+FP4X4 = mybir.dt.float4_e2m1fn_x4
+ALU = mybir.AluOpType
+COPY = mybir.ActivationFunctionType.Copy
+
+P = 128
+PACK = 4
+HALF = J // 2
+CHUNK = 128
+
+
+def tile_list_bounded_columns_pl_kernel(tc, xf, lo, hi, fa, fb, wa_words, wa_scales, wb_words, wb_scales, offs, out_0, out_1, out_2):
+    nc = tc.nc
+    with ExitStack() as ctx:
+        held = ctx.enter_context(tc.tile_pool(name="held", bufs=1))
+        pool = ctx.enter_context(tc.tile_pool(name="pool", bufs=1))
+        psum = ctx.enter_context(tc.psum_pool(name="psum", bufs=1))
+
+        offsets = held.tile([P, J // 16], U16, name="offsets")
+        wa_raw = pool.tile([P, N], I32, name="wa_raw")
+        wb_raw = pool.tile([P, 2 * N], U8, name="wb_raw")
+        ws_raw = pool.tile([P, N], U8, name="ws_raw")
+        planes = [pool.tile([P, T], F32, name="plane%d" % t) for t in range(PACK)]
+        xf_planes = xf.rearrange("(p t) c -> t p c", t=PACK)
+
+        nc.vector.memset(ws_raw[:].bitcast(I32), 0)
+        warm = pool.tile([P, 8], F32, name="warm")
+        warm2 = pool.tile([P, 8], F32, name="warm2")
+        nc.vector.memset(warm[:], 0.0)
+        nc.scalar.activation(warm2[:], warm[:], COPY)
+
+        def load_scale_rows(queue, src, first_row, r):
+            queue.dma_start(ws_raw[first_row + r : P : 32, :].bitcast(I32), src[0, r:16:4, :].bitcast(I32))
+
+        per_feature = {}
+        nc.sync.dma_start(wa_raw[:], wa_words[0].rearrange("p n t -> p (n t)").bitcast(I32))
+        nc.sync.dma_start(wb_raw[:].bitcast(I32), wb_words[0].bitcast(I32))
+        nc.sync.dma_start(planes[0][:], xf_planes[0])
+        nc.sync.dma_start(offsets[:], offs)
+        for name, src in (("hi", hi), ("lo", lo), ("fa", fa), ("fb", fb)):
+            per_feature[name] = pool.tile([P, PACK], F32, name=name + "_sb")
+            nc.sync.dma_start(per_feature[name][:], src.rearrange("(p t) o -> p (t o)", t=PACK))
+        nc.sync.dma_start(planes[1][:], xf_planes[1])
+        nc.sync.dma_start(planes[2][:], xf_planes[2])
+        for r in range(4):
+            load_scale_rows(nc.sync, wa_scales, 4, r)
+        for r in range(4):
+            load_scale_rows(nc.sync if r < 2 else nc.gpsimd, wb_scales, 0, r)
+        nc.sync.dma_start(planes[3][:], xf_planes[3])
+
+        wa_dealt = pool.tile([P, N], I32, name="wa_dealt", align_bytes=64)
+        wb_dealt = pool.tile([P, 2 * N], U8, name="wb_dealt", align_bytes=64)
+        ws_dealt = pool.tile([P, N], U8, name="ws_dealt", align_bytes=64)
+        nc.vector.tensor_copy(wa_dealt[:].rearrange("p (t m) -> p t m", t=PACK), wa_raw[:].rearrange("p (m t) -> p t m", t=PACK))
+        nc.vector.tensor_copy(
+            wb_dealt[:].rearrange("p (t m e) -> p t m e", t=PACK, e=2), wb_raw[:].rearrange("p (m t e) -> p t m e", t=PACK, e=2)
+        )
+
+        pairs = {op: [pool.tile([P, 2, HALF, 2], BF16, name="pairs_%s%d" % (op, h)) for h in range(2)] for op in "ac"}
+
+        def bound(t, j0, width):
+            picked = pool.tile([P, width], F32, name="picked%d_%d" % (t, j0))
+            kept = pool.tile([P, width], F32, name="kept%d_%d" % (t, j0))
+            cut = pool.tile([P, width], F32, name="cut%d_%d" % (t, j0))
+            nc.vector.tensor_copy(picked[:], planes[t][:].indirect(offsets[:, j0 // 16 : (j0 + width) // 16]))
+            nc.vector.tensor_scalar(
+                kept[:], picked[:], per_feature["hi"][:, t : t + 1], per_feature["lo"][:, t : t + 1], ALU.min, ALU.max
+            )
+            nc.vector.tensor_tensor(cut[:], picked[:], kept[:], ALU.subtract)
+            for op, src, factor in (("a", kept, "fa"), ("c", cut, "fb")):
+                for c0 in range(0, width, HALF):
+                    h = (j0 + c0) // HALF
+                    nc.scalar.activation(
+                        pairs[op][h][:, t // 2, :, t % 2], src[:, c0 : c0 + HALF], COPY, scale=per_feature[factor][:, t : t + 1]
+                    )
+
+        for t in range(PACK - 1):
+            bound(t, 0, J)
+        nc.vector.tensor_copy(ws_dealt[:].rearrange("p (t m) -> p t m", t=PACK), ws_raw[:].rearrange("p (m t) -> p t m", t=PACK))
+        codes = {}
+        scales = {}
+
+        def quantise(op, h):
+            grouped = pool.tile([P, HALF * PACK], BF16, name="grouped_%s%d" % (op, h), align_bytes=64)
+            words = pairs[op][h][:].rearrange("p u j e -> p u (j e)")
+            if (op, h) == ("a", 1):
+                nc.scalar.copy(
+                    grouped[:].bitcast(U32).rearrange("p (j u) -> p j u", u=2), words.bitcast(U32).rearrange("p u j -> p j u")
+                )
+            else:
+                nc.vector.tensor_copy(
+                    grouped[:].bitcast(I32).rearrange("p (j u) -> p j u", u=2), words.bitcast(I32).rearrange("p u j -> p j u")
+                )
+            codes[op, h] = pool.tile([P, HALF], U32, name="codes_%s%d" % (op, h), align_bytes=64)
+            scales[op, h] = pool.tile([P, HALF], U8, name="scales_%s%d" % (op, h), align_bytes=64)
+            nc.vector.quantize_mx(out=codes[op, h][:].bitcast(FP8X4), scales=scales[op, h][:], in_=grouped[:])
+
+        banks = [psum.tile([P, PACK, CHUNK], F32, name="bank%d" % c) for c in range(J // CHUNK)]
+
+        def multiply(c):
+            h, cols = c // 2, slice((c % 2) * CHUNK, (c % 2 + 1) * CHUNK)
+            for t in range(PACK):
+                nc.tensor.matmul_mx(
+                    out=banks[c][:, t, :],
+                    lhsT=wa_dealt[:, t * P : (t + 1) * P].bitcast(FP8X4),
+                    lhsT_scale=ws_dealt[4:P, t * P : (t + 1) * P],
+                    rhs=codes["a", h][:, cols].bitcast(FP8X4),
+                    rhs_scale=scales["a", h][:, cols],
+                    start=(t == 0),
+                    stop=False,
+                )
+            for t in range(PACK):
+                nc.tensor.matmul_mx(
+                    out=banks[c][:, t, :],
+                    lhsT=wb_dealt[:, 2 * t * P : 2 * (t + 1) * P].bitcast(FP4X4),
+                    lhsT_scale=ws_dealt[:, t * P : (t + 1) * P],
+                    rhs=codes["c", h][:, cols].bitcast(FP8X4),
+                    rhs_scale=scales["c", h][:, cols],
+                    start=False,
+                    stop=(t == PACK - 1),
+                )
+
+        y_codes = pool.tile([P, J], U32, name="y_codes", align_bytes=64)
+        y_scales = pool.tile([P, J], U8, name="y_scales", align_bytes=64)
+        y_rows = out_0.rearrange("(p t) j -> p t j", t=PACK)
+        words_out = out_1[0].rearrange("p c r -> p (c r)").bitcast(I32)
+
+        for h in range(2):
+            bound(PACK - 1, h * HALF, HALF)
+            quantise("a", h)
+            quantise("c", h)
+            multiply(2 * h)
+            multiply(2 * h + 1)
+        for c in range(J // CHUNK):
+            cols = slice(c * CHUNK, (c + 1) * CHUNK)
+            y = pool.tile([P, PACK, CHUNK], F32, name="y%d" % c)
+            nc.scalar.copy(y[:], banks[c][:])
+            nc.sync.dma_start(y_rows[:, :, cols], y[:])
+            y_grouped = pool.tile([P, CHUNK * PACK], BF16, name="y_grouped%d" % c, align_bytes=64)
+            nc.vector.tensor_copy(
+                y_grouped[:].rearrange("p (g i t) -> p g t i", i=4, t=PACK), y[:].rearrange("p t (g i) -> p g t i", i=4)
+            )
+            nc.vector.quantize_mx(out=y_codes[:, cols].bitcast(FP8X4), scales=y_scales[:, cols], in_=y_grouped[:])
+            if c % 2 == 1:
+                half = slice((c - 1) * CHUNK, (c + 1) * CHUNK)
+                nc.sync.dma_start(words_out[:, half], y_codes[:, half].bitcast(I32))
+        for q in range(4):
+            queue = nc.sync if q < 2 else nc.scalar
+            queue.dma_start(out_2[0, 4 * q : 4 * q + 4, :].bitcast(I32), y_scales[32 * q : 32 * q + 4, :].bitcast(I32))

@@ -1,6 +1,7 @@
 from contextlib import ExitStack
 
 import concourse.mybir as mybir
+from concourse.masks import make_identity
 
 K, T, J, N = 512, 2048, 512, 512
 FLOPS = 2 * 2 * K * N * J
@@ -37,29 +38,38 @@ def tile_list_bounded_columns_pl_kernel(tc, xf, lo, hi, fa, fb, wa_words, wa_sca
         xf_planes = xf.rearrange("(p t) c -> t p c", t=PACK)
 
         nc.vector.memset(ws_raw[:].bitcast(I32), 0)
-        warm = pool.tile([P, 8], F32, name="warm")
-        warm2 = pool.tile([P, 8], F32, name="warm2")
-        nc.vector.memset(warm[:], 0.0)
-        nc.scalar.activation(warm2[:], warm[:], COPY)
+
 
         def load_scale_rows(queue, src, first_row, r):
             queue.dma_start(ws_raw[first_row + r : P : 32, :].bitcast(I32), src[0, r:16:4, :].bitcast(I32))
 
         per_feature = {}
+
+        def load_per_feature(queue, name, src):
+            per_feature[name] = pool.tile([P, PACK], F32, name=name + "_sb")
+            queue.dma_start(per_feature[name][:], src.rearrange("(p t) o -> p (t o)", t=PACK))
+
+        load_per_feature(nc.scalar, "fa", fa)
+        load_per_feature(nc.scalar, "fb", fb)
         nc.sync.dma_start(wa_raw[:], wa_words[0].rearrange("p n t -> p (n t)").bitcast(I32))
         nc.sync.dma_start(wb_raw[:].bitcast(I32), wb_words[0].bitcast(I32))
         nc.sync.dma_start(planes[0][:], xf_planes[0])
         nc.sync.dma_start(offsets[:], offs)
-        for name, src in (("hi", hi), ("lo", lo), ("fa", fa), ("fb", fb)):
-            per_feature[name] = pool.tile([P, PACK], F32, name=name + "_sb")
-            nc.sync.dma_start(per_feature[name][:], src.rearrange("(p t) o -> p (t o)", t=PACK))
+        load_per_feature(nc.sync, "hi", hi)
+        load_per_feature(nc.sync, "lo", lo)
         nc.sync.dma_start(planes[1][:], xf_planes[1])
+        for r in range(2):
+            load_scale_rows(nc.sync, wa_scales, 4, r)
         nc.sync.dma_start(planes[2][:], xf_planes[2])
-        for r in range(4):
+        for r in range(2, 4):
             load_scale_rows(nc.sync, wa_scales, 4, r)
         for r in range(4):
-            load_scale_rows(nc.sync if r < 2 else nc.gpsimd, wb_scales, 0, r)
+            load_scale_rows(nc.sync, wb_scales, 0, r)
         nc.sync.dma_start(planes[3][:], xf_planes[3])
+        warm = pool.tile([P, 8], F32, name="warm")
+        warm2 = pool.tile([P, 8], F32, name="warm2")
+        nc.vector.memset(warm[:], 0.0)
+        nc.scalar.activation(warm2[:], warm[:], COPY)
 
         wa_dealt = pool.tile([P, N], I32, name="wa_dealt", align_bytes=64)
         wb_dealt = pool.tile([P, 2 * N], U8, name="wb_dealt", align_bytes=64)
@@ -79,17 +89,19 @@ def tile_list_bounded_columns_pl_kernel(tc, xf, lo, hi, fa, fb, wa_words, wa_sca
             nc.vector.tensor_scalar(
                 kept[:], picked[:], per_feature["hi"][:, t : t + 1], per_feature["lo"][:, t : t + 1], ALU.min, ALU.max
             )
-            nc.vector.tensor_tensor(cut[:], picked[:], kept[:], ALU.subtract)
+            (nc.gpsimd if t < PACK - 1 else nc.vector).tensor_tensor(cut[:], picked[:], kept[:], ALU.subtract)
             for op, src, factor in (("a", kept, "fa"), ("c", cut, "fb")):
                 for c0 in range(0, width, HALF):
                     h = (j0 + c0) // HALF
                     nc.scalar.activation(
                         pairs[op][h][:, t // 2, :, t % 2], src[:, c0 : c0 + HALF], COPY, scale=per_feature[factor][:, t : t + 1]
                     )
+            return kept
 
         for t in range(PACK - 1):
             bound(t, 0, J)
         nc.vector.tensor_copy(ws_dealt[:].rearrange("p (t m) -> p t m", t=PACK), ws_raw[:].rearrange("p (m t) -> p t m", t=PACK))
+
         codes = {}
         scales = {}
 
@@ -138,8 +150,27 @@ def tile_list_bounded_columns_pl_kernel(tc, xf, lo, hi, fa, fb, wa_words, wa_sca
         y_rows = out_0.rearrange("(p t) j -> p t j", t=PACK)
         words_out = out_1[0].rearrange("p c r -> p (c r)").bitcast(I32)
 
+        identity = pool.tile([P, P], F32, name="identity")
+        make_identity(nc, identity[:])
+        warm_bank = psum.tile([P, N], F32, name="warm_bank")
+
+        def warm_tensor(trigger):
+            nc.tensor.transpose(warm_bank[:, 0:P], trigger[:, 0:P], identity[:])
+            for repeat in range(2):
+                nc.tensor.matmul_mx(
+                    out=warm_bank[:],
+                    lhsT=wa_dealt[:, 0:P].bitcast(FP8X4),
+                    lhsT_scale=ws_dealt[4:P, 0:P],
+                    rhs=wa_dealt[:].bitcast(FP8X4),
+                    rhs_scale=ws_dealt[4:P, :],
+                    start=True,
+                    stop=True,
+                )
+
         for h in range(2):
-            bound(PACK - 1, h * HALF, HALF)
+            kept = bound(PACK - 1, h * HALF, HALF)
+            if h == 0:
+                warm_tensor(kept)
             quantise("a", h)
             quantise("c", h)
             multiply(2 * h)

@@ -19,35 +19,40 @@ COPY = mybir.ActivationFunctionType.Copy
 
 P = 128
 PACK = 4
+QUADRANT = 32
+OFFSETS_A_COLUMN = 16
 HALF = J // 2
 CHUNK = 128
+WA_SCALE_ROW = 4
+
+PIECES = {"xa": [(0, CHUNK), (CHUNK, CHUNK), (HALF, HALF)], "xc": [(0, HALF), (HALF, HALF)]}
 
 
-def tile_list_bounded_columns_pl_kernel(tc, xf, lo, hi, fa, fb, wa_words, wa_scales, wb_words, wb_scales, offs, out_0, out_1, out_2):
+def tile_list_bounded_columns_pl_kernel(
+    tc, xf, lo, hi, fa, fb, wa_words, wa_scales, wb_words, wb_scales, offs, out_0, out_1, out_2
+):
     nc = tc.nc
     with ExitStack() as ctx:
         held = ctx.enter_context(tc.tile_pool(name="held", bufs=1))
         pool = ctx.enter_context(tc.tile_pool(name="pool", bufs=1))
         psum = ctx.enter_context(tc.psum_pool(name="psum", bufs=1))
 
-        offsets = held.tile([P, J // 16], U16, name="offsets")
+        offsets = held.tile([P, J // OFFSETS_A_COLUMN], U16, name="offsets")
         wa_raw = pool.tile([P, N], I32, name="wa_raw")
         wb_raw = pool.tile([P, 2 * N], U8, name="wb_raw")
-        ws_raw = pool.tile([P, N], U8, name="ws_raw")
+        scales_raw = pool.tile([P, N], U8, name="scales_raw")
         planes = [pool.tile([P, T], F32, name="plane%d" % t) for t in range(PACK)]
         xf_planes = xf.rearrange("(p t) c -> t p c", t=PACK)
-
-        nc.vector.memset(ws_raw[:].bitcast(I32), 0)
-
-
-        def load_scale_rows(queue, src, first_row, r):
-            queue.dma_start(ws_raw[first_row + r : P : 32, :].bitcast(I32), src[0, r:16:4, :].bitcast(I32))
-
         per_feature = {}
 
         def load_per_feature(queue, name, src):
             per_feature[name] = pool.tile([P, PACK], F32, name=name + "_sb")
             queue.dma_start(per_feature[name][:], src.rearrange("(p t) o -> p (t o)", t=PACK))
+
+        def load_scale_rows(src, first_row, r):
+            nc.sync.dma_start(scales_raw[first_row + r : P : QUADRANT, :].bitcast(I32), src[0, r:16:4, :].bitcast(I32))
+
+        nc.vector.memset(scales_raw[:].bitcast(I32), 0)
 
         load_per_feature(nc.scalar, "fa", fa)
         load_per_feature(nc.scalar, "fb", fb)
@@ -59,78 +64,93 @@ def tile_list_bounded_columns_pl_kernel(tc, xf, lo, hi, fa, fb, wa_words, wa_sca
         load_per_feature(nc.sync, "lo", lo)
         nc.sync.dma_start(planes[1][:], xf_planes[1])
         for r in range(2):
-            load_scale_rows(nc.sync, wa_scales, 4, r)
+            load_scale_rows(wa_scales, WA_SCALE_ROW, r)
         nc.sync.dma_start(planes[2][:], xf_planes[2])
         for r in range(2, 4):
-            load_scale_rows(nc.sync, wa_scales, 4, r)
+            load_scale_rows(wa_scales, WA_SCALE_ROW, r)
         for r in range(4):
-            load_scale_rows(nc.sync, wb_scales, 0, r)
+            load_scale_rows(wb_scales, 0, r)
         nc.sync.dma_start(planes[3][:], xf_planes[3])
-        warm = pool.tile([P, 8], F32, name="warm")
-        warm2 = pool.tile([P, 8], F32, name="warm2")
-        nc.vector.memset(warm[:], 0.0)
-        nc.scalar.activation(warm2[:], warm[:], COPY)
+
+        warm_in = pool.tile([P, 8], F32, name="warm_in")
+        warm_out = pool.tile([P, 8], F32, name="warm_out")
+        nc.vector.memset(warm_in[:], 0.0)
+        nc.scalar.activation(warm_out[:], warm_in[:], COPY)
 
         wa_dealt = pool.tile([P, N], I32, name="wa_dealt", align_bytes=64)
         wb_dealt = pool.tile([P, 2 * N], U8, name="wb_dealt", align_bytes=64)
-        ws_dealt = pool.tile([P, N], U8, name="ws_dealt", align_bytes=64)
-        nc.vector.tensor_copy(wa_dealt[:].rearrange("p (t m) -> p t m", t=PACK), wa_raw[:].rearrange("p (m t) -> p t m", t=PACK))
+        scales_dealt = pool.tile([P, N], U8, name="scales_dealt", align_bytes=64)
         nc.vector.tensor_copy(
-            wb_dealt[:].rearrange("p (t m e) -> p t m e", t=PACK, e=2), wb_raw[:].rearrange("p (m t e) -> p t m e", t=PACK, e=2)
+            wa_dealt[:].rearrange("p (t m) -> p t m", t=PACK), wa_raw[:].rearrange("p (m t) -> p t m", t=PACK)
+        )
+        nc.vector.tensor_copy(
+            wb_dealt[:].rearrange("p (t m e) -> p t m e", t=PACK, e=2),
+            wb_raw[:].rearrange("p (m t e) -> p t m e", t=PACK, e=2),
         )
 
-        pairs = {op: [pool.tile([P, 2, HALF, 2], BF16, name="pairs_%s%d" % (op, h)) for h in range(2)] for op in "ac"}
+        pairs = {
+            (operand, j0): pool.tile([P, 2, width, 2], BF16, name="pairs_%s%d" % (operand, j0))
+            for operand in PIECES
+            for j0, width in PIECES[operand]
+        }
 
-        def bound(t, j0, width):
+        def scale(operand, factor, t, src, src_j0, src_width):
+            for j0, width in PIECES[operand]:
+                if src_j0 <= j0 < src_j0 + src_width:
+                    nc.scalar.activation(
+                        pairs[operand, j0][:, t // 2, :, t % 2],
+                        src[:, j0 - src_j0 : j0 - src_j0 + width],
+                        COPY,
+                        scale=per_feature[factor][:, t : t + 1],
+                    )
+
+        def bound(t, j0, width, subtracting_engine):
             picked = pool.tile([P, width], F32, name="picked%d_%d" % (t, j0))
             kept = pool.tile([P, width], F32, name="kept%d_%d" % (t, j0))
-            cut = pool.tile([P, width], F32, name="cut%d_%d" % (t, j0))
-            nc.vector.tensor_copy(picked[:], planes[t][:].indirect(offsets[:, j0 // 16 : (j0 + width) // 16]))
+            listed = offsets[:, j0 // OFFSETS_A_COLUMN : (j0 + width) // OFFSETS_A_COLUMN]
+            nc.vector.tensor_copy(picked[:], planes[t][:].indirect(listed))
             nc.vector.tensor_scalar(
                 kept[:], picked[:], per_feature["hi"][:, t : t + 1], per_feature["lo"][:, t : t + 1], ALU.min, ALU.max
             )
-            (nc.gpsimd if t < PACK - 1 else nc.vector).tensor_tensor(cut[:], picked[:], kept[:], ALU.subtract)
-            for op, src, factor in (("a", kept, "fa"), ("c", cut, "fb")):
-                for c0 in range(0, width, HALF):
-                    h = (j0 + c0) // HALF
-                    nc.scalar.activation(
-                        pairs[op][h][:, t // 2, :, t % 2], src[:, c0 : c0 + HALF], COPY, scale=per_feature[factor][:, t : t + 1]
-                    )
+            for c0 in range(0, width, HALF):
+                cols = slice(c0, c0 + HALF)
+                cut = pool.tile([P, HALF], F32, name="cut%d_%d" % (t, j0 + c0))
+                subtracting_engine.tensor_tensor(cut[:], picked[:, cols], kept[:, cols], ALU.subtract)
+                scale("xa", "fa", t, kept[:, cols], j0 + c0, HALF)
+                scale("xc", "fb", t, cut[:], j0 + c0, HALF)
             return kept
 
         for t in range(PACK - 1):
-            bound(t, 0, J)
-        nc.vector.tensor_copy(ws_dealt[:].rearrange("p (t m) -> p t m", t=PACK), ws_raw[:].rearrange("p (m t) -> p t m", t=PACK))
+            bound(t, 0, J, nc.gpsimd)
+        nc.vector.tensor_copy(
+            scales_dealt[:].rearrange("p (t m) -> p t m", t=PACK), scales_raw[:].rearrange("p (m t) -> p t m", t=PACK)
+        )
 
         codes = {}
         scales = {}
 
-        def quantise(op, h):
-            grouped = pool.tile([P, HALF * PACK], BF16, name="grouped_%s%d" % (op, h), align_bytes=64)
-            words = pairs[op][h][:].rearrange("p u j e -> p u (j e)")
-            if (op, h) == ("a", 1):
-                nc.scalar.copy(
-                    grouped[:].bitcast(U32).rearrange("p (j u) -> p j u", u=2), words.bitcast(U32).rearrange("p u j -> p j u")
-                )
-            else:
-                nc.vector.tensor_copy(
-                    grouped[:].bitcast(I32).rearrange("p (j u) -> p j u", u=2), words.bitcast(I32).rearrange("p u j -> p j u")
-                )
-            codes[op, h] = pool.tile([P, HALF], U32, name="codes_%s%d" % (op, h), align_bytes=64)
-            scales[op, h] = pool.tile([P, HALF], U8, name="scales_%s%d" % (op, h), align_bytes=64)
-            nc.vector.quantize_mx(out=codes[op, h][:].bitcast(FP8X4), scales=scales[op, h][:], in_=grouped[:])
+        def quantise(operand, j0, width):
+            grouped = pool.tile([P, width * PACK], BF16, name="grouped_%s%d" % (operand, j0), align_bytes=64)
+            words = pairs[operand, j0][:].rearrange("p u j e -> p u (j e)")
+            copy, word = (nc.scalar.copy, U32) if (operand, j0) == ("xa", HALF) else (nc.vector.tensor_copy, I32)
+            copy(grouped[:].bitcast(word).rearrange("p (j u) -> p j u", u=2), words.bitcast(word).rearrange("p u j -> p j u"))
+            piece_codes = pool.tile([P, width], U32, name="codes_%s%d" % (operand, j0), align_bytes=64)
+            piece_scales = pool.tile([P, width], U8, name="scales_%s%d" % (operand, j0), align_bytes=64)
+            nc.vector.quantize_mx(out=piece_codes[:].bitcast(FP8X4), scales=piece_scales[:], in_=grouped[:])
+            for c0 in range(0, width, CHUNK):
+                codes[operand, (j0 + c0) // CHUNK] = piece_codes[:, c0 : c0 + CHUNK]
+                scales[operand, (j0 + c0) // CHUNK] = piece_scales[:, c0 : c0 + CHUNK]
 
         banks = [psum.tile([P, PACK, CHUNK], F32, name="bank%d" % c) for c in range(J // CHUNK)]
 
         def multiply(c):
-            h, cols = c // 2, slice((c % 2) * CHUNK, (c % 2 + 1) * CHUNK)
             for t in range(PACK):
                 nc.tensor.matmul_mx(
                     out=banks[c][:, t, :],
                     lhsT=wa_dealt[:, t * P : (t + 1) * P].bitcast(FP8X4),
-                    lhsT_scale=ws_dealt[4:P, t * P : (t + 1) * P],
-                    rhs=codes["a", h][:, cols].bitcast(FP8X4),
-                    rhs_scale=scales["a", h][:, cols],
+                    lhsT_scale=scales_dealt[WA_SCALE_ROW:P, t * P : (t + 1) * P],
+                    rhs=codes["xa", c].bitcast(FP8X4),
+                    rhs_scale=scales["xa", c],
                     start=(t == 0),
                     stop=False,
                 )
@@ -138,43 +158,45 @@ def tile_list_bounded_columns_pl_kernel(tc, xf, lo, hi, fa, fb, wa_words, wa_sca
                 nc.tensor.matmul_mx(
                     out=banks[c][:, t, :],
                     lhsT=wb_dealt[:, 2 * t * P : 2 * (t + 1) * P].bitcast(FP4X4),
-                    lhsT_scale=ws_dealt[:, t * P : (t + 1) * P],
-                    rhs=codes["c", h][:, cols].bitcast(FP8X4),
-                    rhs_scale=scales["c", h][:, cols],
+                    lhsT_scale=scales_dealt[:, t * P : (t + 1) * P],
+                    rhs=codes["xc", c].bitcast(FP8X4),
+                    rhs_scale=scales["xc", c],
                     start=False,
                     stop=(t == PACK - 1),
                 )
-
-        y_codes = pool.tile([P, J], U32, name="y_codes", align_bytes=64)
-        y_scales = pool.tile([P, J], U8, name="y_scales", align_bytes=64)
-        y_rows = out_0.rearrange("(p t) j -> p t j", t=PACK)
-        words_out = out_1[0].rearrange("p c r -> p (c r)").bitcast(I32)
 
         identity = pool.tile([P, P], F32, name="identity")
         make_identity(nc, identity[:])
         warm_bank = psum.tile([P, N], F32, name="warm_bank")
 
-        def warm_tensor(trigger):
-            nc.tensor.transpose(warm_bank[:, 0:P], trigger[:, 0:P], identity[:])
+        def warm_up_tensor_engine(just_bounded):
+            nc.tensor.transpose(warm_bank[:, 0:P], just_bounded[:, 0:P], identity[:])
             for repeat in range(2):
                 nc.tensor.matmul_mx(
                     out=warm_bank[:],
                     lhsT=wa_dealt[:, 0:P].bitcast(FP8X4),
-                    lhsT_scale=ws_dealt[4:P, 0:P],
+                    lhsT_scale=scales_dealt[WA_SCALE_ROW:P, 0:P],
                     rhs=wa_dealt[:].bitcast(FP8X4),
-                    rhs_scale=ws_dealt[4:P, :],
+                    rhs_scale=scales_dealt[WA_SCALE_ROW:P, :],
                     start=True,
                     stop=True,
                 )
 
-        for h in range(2):
-            kept = bound(PACK - 1, h * HALF, HALF)
-            if h == 0:
-                warm_tensor(kept)
-            quantise("a", h)
-            quantise("c", h)
-            multiply(2 * h)
-            multiply(2 * h + 1)
+        for half_j0 in range(0, J, HALF):
+            kept = bound(PACK - 1, half_j0, HALF, nc.vector)
+            if half_j0 == 0:
+                warm_up_tensor_engine(kept)
+            for operand in PIECES:
+                for j0, width in PIECES[operand]:
+                    if half_j0 <= j0 < half_j0 + HALF:
+                        quantise(operand, j0, width)
+            for c in range(half_j0 // CHUNK, (half_j0 + HALF) // CHUNK):
+                multiply(c)
+
+        y_codes = pool.tile([P, J], U32, name="y_codes", align_bytes=64)
+        y_scales = pool.tile([P, J], U8, name="y_scales", align_bytes=64)
+        y_rows = out_0.rearrange("(p t) j -> p t j", t=PACK)
+        words_out = out_1[0].rearrange("p c r -> p (c r)").bitcast(I32)
         for c in range(J // CHUNK):
             cols = slice(c * CHUNK, (c + 1) * CHUNK)
             y = pool.tile([P, PACK, CHUNK], F32, name="y%d" % c)
@@ -185,9 +207,11 @@ def tile_list_bounded_columns_pl_kernel(tc, xf, lo, hi, fa, fb, wa_words, wa_sca
                 y_grouped[:].rearrange("p (g i t) -> p g t i", i=4, t=PACK), y[:].rearrange("p t (g i) -> p g t i", i=4)
             )
             nc.vector.quantize_mx(out=y_codes[:, cols].bitcast(FP8X4), scales=y_scales[:, cols], in_=y_grouped[:])
-            if c % 2 == 1:
-                half = slice((c - 1) * CHUNK, (c + 1) * CHUNK)
+            if (c + 1) * CHUNK % HALF == 0:
+                half = slice((c + 1) * CHUNK - HALF, (c + 1) * CHUNK)
                 nc.sync.dma_start(words_out[:, half], y_codes[:, half].bitcast(I32))
-        for q in range(4):
+        for q in range(P // QUADRANT):
             queue = nc.sync if q < 2 else nc.scalar
-            queue.dma_start(out_2[0, 4 * q : 4 * q + 4, :].bitcast(I32), y_scales[32 * q : 32 * q + 4, :].bitcast(I32))
+            queue.dma_start(
+                out_2[0, 4 * q : 4 * q + 4, :].bitcast(I32), y_scales[QUADRANT * q : QUADRANT * q + 4, :].bitcast(I32)
+            )

from contextlib import ExitStack

import concourse.mybir as mybir
from concourse.masks import make_identity

K, T, J, N = 512, 2048, 512, 512
FLOPS = 2 * 2 * K * N * J

F32 = mybir.dt.float32
BF16 = mybir.dt.bfloat16
I32 = mybir.dt.int32
U32 = mybir.dt.uint32
U16 = mybir.dt.uint16
U8 = mybir.dt.uint8
FP8X4 = mybir.dt.float8_e4m3fn_x4
FP4X4 = mybir.dt.float4_e2m1fn_x4
ALU = mybir.AluOpType
COPY = mybir.ActivationFunctionType.Copy

P = 128
PACK = 4
QUADRANT = 32
OFFSETS_A_COLUMN = 16
HALF = J // 2
CHUNK = 128
WA_SCALE_ROW = 4

PIECES = {"xa": [(0, CHUNK), (CHUNK, CHUNK), (HALF, HALF)], "xc": [(0, HALF), (HALF, HALF)]}


def tile_list_bounded_columns_pl_kernel(
    tc, xf, lo, hi, fa, fb, wa_words, wa_scales, wb_words, wb_scales, offs, out_0, out_1, out_2
):
    nc = tc.nc
    with ExitStack() as ctx:
        held = ctx.enter_context(tc.tile_pool(name="held", bufs=1))
        pool = ctx.enter_context(tc.tile_pool(name="pool", bufs=1))
        psum = ctx.enter_context(tc.psum_pool(name="psum", bufs=1))

        offsets = held.tile([P, J // OFFSETS_A_COLUMN], U16, name="offsets")
        wa_raw = pool.tile([P, N], I32, name="wa_raw")
        wb_raw = pool.tile([P, 2 * N], U8, name="wb_raw")
        scales_raw = pool.tile([P, N], U8, name="scales_raw")
        planes = [pool.tile([P, T], F32, name="plane%d" % t) for t in range(PACK)]
        xf_planes = xf.rearrange("(p t) c -> t p c", t=PACK)
        per_feature = {}

        def load_per_feature(queue, name, src):
            per_feature[name] = pool.tile([P, PACK], F32, name=name + "_sb")
            queue.dma_start(per_feature[name][:], src.rearrange("(p t) o -> p (t o)", t=PACK))

        def load_scale_rows(src, first_row, r):
            nc.sync.dma_start(scales_raw[first_row + r : P : QUADRANT, :].bitcast(I32), src[0, r:16:4, :].bitcast(I32))

        nc.vector.memset(scales_raw[:].bitcast(I32), 0)

        load_per_feature(nc.scalar, "fa", fa)
        load_per_feature(nc.scalar, "fb", fb)
        nc.sync.dma_start(wa_raw[:], wa_words[0].rearrange("p n t -> p (n t)").bitcast(I32))
        nc.sync.dma_start(wb_raw[:].bitcast(I32), wb_words[0].bitcast(I32))
        nc.sync.dma_start(planes[0][:], xf_planes[0])
        nc.sync.dma_start(offsets[:], offs)
        load_per_feature(nc.sync, "hi", hi)
        load_per_feature(nc.sync, "lo", lo)
        nc.sync.dma_start(planes[1][:], xf_planes[1])
        for r in range(2):
            load_scale_rows(wa_scales, WA_SCALE_ROW, r)
        nc.sync.dma_start(planes[2][:], xf_planes[2])
        for r in range(2, 4):
            load_scale_rows(wa_scales, WA_SCALE_ROW, r)
        for r in range(4):
            load_scale_rows(wb_scales, 0, r)
        nc.sync.dma_start(planes[3][:], xf_planes[3])

        warm_in = pool.tile([P, 8], F32, name="warm_in")
        warm_out = pool.tile([P, 8], F32, name="warm_out")
        nc.vector.memset(warm_in[:], 0.0)
        nc.scalar.activation(warm_out[:], warm_in[:], COPY)

        wa_dealt = pool.tile([P, N], I32, name="wa_dealt", align_bytes=64)
        wb_dealt = pool.tile([P, 2 * N], U8, name="wb_dealt", align_bytes=64)
        scales_dealt = pool.tile([P, N], U8, name="scales_dealt", align_bytes=64)
        nc.vector.tensor_copy(
            wa_dealt[:].rearrange("p (t m) -> p t m", t=PACK), wa_raw[:].rearrange("p (m t) -> p t m", t=PACK)
        )
        nc.vector.tensor_copy(
            wb_dealt[:].rearrange("p (t m e) -> p t m e", t=PACK, e=2),
            wb_raw[:].rearrange("p (m t e) -> p t m e", t=PACK, e=2),
        )

        pairs = {
            (operand, j0): pool.tile([P, 2, width, 2], BF16, name="pairs_%s%d" % (operand, j0))
            for operand in PIECES
            for j0, width in PIECES[operand]
        }

        def scale(operand, factor, t, src, src_j0, src_width):
            for j0, width in PIECES[operand]:
                if src_j0 <= j0 < src_j0 + src_width:
                    nc.scalar.activation(
                        pairs[operand, j0][:, t // 2, :, t % 2],
                        src[:, j0 - src_j0 : j0 - src_j0 + width],
                        COPY,
                        scale=per_feature[factor][:, t : t + 1],
                    )

        def bound(t, j0, width, subtracting_engine):
            picked = pool.tile([P, width], F32, name="picked%d_%d" % (t, j0))
            kept = pool.tile([P, width], F32, name="kept%d_%d" % (t, j0))
            listed = offsets[:, j0 // OFFSETS_A_COLUMN : (j0 + width) // OFFSETS_A_COLUMN]
            nc.vector.tensor_copy(picked[:], planes[t][:].indirect(listed))
            nc.vector.tensor_scalar(
                kept[:], picked[:], per_feature["hi"][:, t : t + 1], per_feature["lo"][:, t : t + 1], ALU.min, ALU.max
            )
            for c0 in range(0, width, HALF):
                cols = slice(c0, c0 + HALF)
                cut = pool.tile([P, HALF], F32, name="cut%d_%d" % (t, j0 + c0))
                subtracting_engine.tensor_tensor(cut[:], picked[:, cols], kept[:, cols], ALU.subtract)
                scale("xa", "fa", t, kept[:, cols], j0 + c0, HALF)
                scale("xc", "fb", t, cut[:], j0 + c0, HALF)
            return kept

        for t in range(PACK - 1):
            bound(t, 0, J, nc.gpsimd)
        nc.vector.tensor_copy(
            scales_dealt[:].rearrange("p (t m) -> p t m", t=PACK), scales_raw[:].rearrange("p (m t) -> p t m", t=PACK)
        )

        codes = {}
        scales = {}

        def quantise(operand, j0, width):
            grouped = pool.tile([P, width * PACK], BF16, name="grouped_%s%d" % (operand, j0), align_bytes=64)
            words = pairs[operand, j0][:].rearrange("p u j e -> p u (j e)")
            copy, word = (nc.scalar.copy, U32) if (operand, j0) == ("xa", HALF) else (nc.vector.tensor_copy, I32)
            copy(grouped[:].bitcast(word).rearrange("p (j u) -> p j u", u=2), words.bitcast(word).rearrange("p u j -> p j u"))
            piece_codes = pool.tile([P, width], U32, name="codes_%s%d" % (operand, j0), align_bytes=64)
            piece_scales = pool.tile([P, width], U8, name="scales_%s%d" % (operand, j0), align_bytes=64)
            nc.vector.quantize_mx(out=piece_codes[:].bitcast(FP8X4), scales=piece_scales[:], in_=grouped[:])
            for c0 in range(0, width, CHUNK):
                codes[operand, (j0 + c0) // CHUNK] = piece_codes[:, c0 : c0 + CHUNK]
                scales[operand, (j0 + c0) // CHUNK] = piece_scales[:, c0 : c0 + CHUNK]

        banks = [psum.tile([P, PACK, CHUNK], F32, name="bank%d" % c) for c in range(J // CHUNK)]

        def multiply(c):
            for t in range(PACK):
                nc.tensor.matmul_mx(
                    out=banks[c][:, t, :],
                    lhsT=wa_dealt[:, t * P : (t + 1) * P].bitcast(FP8X4),
                    lhsT_scale=scales_dealt[WA_SCALE_ROW:P, t * P : (t + 1) * P],
                    rhs=codes["xa", c].bitcast(FP8X4),
                    rhs_scale=scales["xa", c],
                    start=(t == 0),
                    stop=False,
                )
            for t in range(PACK):
                nc.tensor.matmul_mx(
                    out=banks[c][:, t, :],
                    lhsT=wb_dealt[:, 2 * t * P : 2 * (t + 1) * P].bitcast(FP4X4),
                    lhsT_scale=scales_dealt[:, t * P : (t + 1) * P],
                    rhs=codes["xc", c].bitcast(FP8X4),
                    rhs_scale=scales["xc", c],
                    start=False,
                    stop=(t == PACK - 1),
                )

        identity = pool.tile([P, P], F32, name="identity")
        make_identity(nc, identity[:])
        warm_bank = psum.tile([P, N], F32, name="warm_bank")

        def warm_up_tensor_engine(just_bounded):
            nc.tensor.transpose(warm_bank[:, 0:P], just_bounded[:, 0:P], identity[:])
            for repeat in range(2):
                nc.tensor.matmul_mx(
                    out=warm_bank[:],
                    lhsT=wa_dealt[:, 0:P].bitcast(FP8X4),
                    lhsT_scale=scales_dealt[WA_SCALE_ROW:P, 0:P],
                    rhs=wa_dealt[:].bitcast(FP8X4),
                    rhs_scale=scales_dealt[WA_SCALE_ROW:P, :],
                    start=True,
                    stop=True,
                )

        for half_j0 in range(0, J, HALF):
            kept = bound(PACK - 1, half_j0, HALF, nc.vector)
            if half_j0 == 0:
                warm_up_tensor_engine(kept)
            for operand in PIECES:
                for j0, width in PIECES[operand]:
                    if half_j0 <= j0 < half_j0 + HALF:
                        quantise(operand, j0, width)
            for c in range(half_j0 // CHUNK, (half_j0 + HALF) // CHUNK):
                multiply(c)

        y_codes = pool.tile([P, J], U32, name="y_codes", align_bytes=64)
        y_scales = pool.tile([P, J], U8, name="y_scales", align_bytes=64)
        y_rows = out_0.rearrange("(p t) j -> p t j", t=PACK)
        words_out = out_1[0].rearrange("p c r -> p (c r)").bitcast(I32)
        for c in range(J // CHUNK):
            cols = slice(c * CHUNK, (c + 1) * CHUNK)
            y = pool.tile([P, PACK, CHUNK], F32, name="y%d" % c)
            nc.scalar.copy(y[:], banks[c][:])
            nc.sync.dma_start(y_rows[:, :, cols], y[:])
            y_grouped = pool.tile([P, CHUNK * PACK], BF16, name="y_grouped%d" % c, align_bytes=64)
            nc.vector.tensor_copy(
                y_grouped[:].rearrange("p (g i t) -> p g t i", i=4, t=PACK), y[:].rearrange("p t (g i) -> p g t i", i=4)
            )
            nc.vector.quantize_mx(out=y_codes[:, cols].bitcast(FP8X4), scales=y_scales[:, cols], in_=y_grouped[:])
            if (c + 1) * CHUNK % HALF == 0:
                half = slice((c + 1) * CHUNK - HALF, (c + 1) * CHUNK)
                nc.sync.dma_start(words_out[:, half], y_codes[:, half].bitcast(I32))
        for q in range(P // QUADRANT):
            queue = nc.sync if q < 2 else nc.scalar
            queue.dma_start(
                out_2[0, 4 * q : 4 * q + 4, :].bitcast(I32), y_scales[QUADRANT * q : QUADRANT * q + 4, :].bitcast(I32)
            )
